import numpy as np
import ml_dtypes


def mxq(x, axis, fmt="e4m3"):
    dtype, down = {"e4m3": (ml_dtypes.float8_e4m3fn, 7), "e5m2": (ml_dtypes.float8_e5m2, 14)}[fmt]
    v = np.moveaxis(np.asarray(x, np.float32).astype(ml_dtypes.bfloat16).astype(np.float64), axis, -1)
    blocks = v.reshape(v.shape[:-1] + (-1, 32))
    amax = np.abs(blocks).max(-1, keepdims=True)
    byte = np.maximum(np.where(amax > 0, np.frexp(amax)[1] - 1 + 127, 0) - down, 1)
    scale = np.exp2(byte - 127.0)
    codes = (blocks / scale).astype(np.float32).astype(dtype).astype(np.float64)
    return np.moveaxis((codes * scale).reshape(v.shape), -1, axis)


WIDE = False


def mx_kscale(k):
    if not WIDE:
        return np.ones(k)
    levels = np.array([10, -10, 5, -5, 0])
    if k % 512:
        return np.exp2(np.random.permutation(np.resize(levels, k // 32))).repeat(32)
    a = np.empty((k // 512, 16))
    for p in range(k // 512):
        a[p, :8] = np.random.permutation(np.resize(levels, 8))
        for g in range(8):
            far = levels[np.abs(levels - a[p, g]) >= 10]
            a[p, g + 8] = far[np.random.randint(len(far))]
    return np.exp2(a.ravel()).repeat(32)


def f64(x):
    return np.asarray(x).astype(np.float64)


def striped8(idx):
    return np.concatenate([x.reshape(-1, 16).T for x in idx]).astype(np.uint16)


def runs(offs, k):
    lists = np.stack([offs[16 * r : 16 * r + 16].T.reshape(-1) for r in range(8)]).astype(np.int64)
    return lists[np.arange(k) % 512 // 64]


def pack_weight(w):
    k, n = w.shape
    w = f64(np.asarray(w, np.float32).astype(ml_dtypes.bfloat16)).reshape(k // 32, 32, n)
    amax = np.abs(w).max(1)
    byte = np.clip(np.where(amax > 0, np.frexp(amax)[1] - 1 + 127 - 7, 1), 1, 254)
    scaled = (w * np.exp2(127.0 - byte)[:, None, :]).reshape(k, n).astype(np.float32)
    words = np.ascontiguousarray(scaled.reshape(k // 512, 128, 4, n).transpose(0, 1, 3, 2)).astype(ml_dtypes.float8_e4m3fn).view(np.uint8)
    return words, np.ascontiguousarray(byte.astype(np.uint8).reshape(k // 512, 16, n))


def unpack_weight(words, scales):
    g, p, n, _ = words.shape
    vals = np.ascontiguousarray(words).view(ml_dtypes.float8_e4m3fn).astype(np.float64) * np.repeat(np.exp2(scales.astype(np.float64) - 127.0), 8, axis=1)[..., None]
    return vals.transpose(0, 1, 3, 2).reshape(g * 512, n)


def sigmoid(v):
    return 1.0 / (1.0 + np.exp(-np.maximum(v, -700.0)))


K, T, S, V, N, G, H = 512, 2048, 512, 256, 512, 2048, 512


def setup_inputs():
    n = np.random.standard_normal
    s = mx_kscale(K)[:, None]
    u = mx_kscale(S)
    packed_xT = pack_weight(n((K, T)) * s)
    packed_dT = pack_weight(n((K, G)) / s)
    return {
        "x_words": packed_xT[0],
        "x_scales": packed_xT[1],
        "d_words": packed_dT[0],
        "d_scales": packed_dT[1],
        "gn": (np.random.uniform(0.5, 1.5, (H, 1)) * u[:, None]).astype(np.float32),
        "w1": (n((H, N)) / np.sqrt(H) / u[:, None]).astype(np.float32),
        "tau": np.random.uniform(0.3, 0.9, (N, 1)).astype(np.float32),
        "tau2": np.random.uniform(0.3, 0.9, (N, 1)).astype(np.float32),
        "offs": striped8(np.random.randint(0, T, (8, S))),
        "k1": striped8(np.random.randint(0, G, (8, H))),
        "n1": striped8(np.stack([np.random.permutation(S) for _ in range(8)])),
        "n2": striped8(np.stack([np.random.permutation(V) for _ in range(8)])),
        "n3": striped8(np.stack([np.random.permutation(V) for _ in range(8)])),
    }


def reference(x_words, x_scales, d_words, d_scales, gn, w1, tau, tau2, offs, k1, n1, n2, n3):
    d_k1 = unpack_weight(d_words, d_scales)[np.arange(K)[:, None], runs(k1, K)]
    xq = unpack_weight(x_words, x_scales)[np.arange(K)[:, None], runs(offs, K)]
    h = 0.0625 * (d_k1.T @ xq)
    ln = h[np.arange(H)[:, None], runs(n1, H)]
    mx = ln.reshape(H, V, 2).max(axis=2)
    mn = ln.reshape(H, V, 2).min(axis=2)
    z = f64(gn) * (mx * sigmoid(mn))
    h2 = mxq(f64(w1), 0, "e4m3").T @ mxq(z, 0, "e4m3")
    top = h2.max(axis=1, keepdims=True)
    ea = np.exp(f64(tau) * (h2[np.arange(N)[:, None], runs(n2, N)] - top))
    low = h2.min(axis=1, keepdims=True)
    ea2 = np.exp(f64(tau2) * (low - (h2[np.arange(N)[:, None], runs(n3, N)])))
    return 1.5 * (h2 * (ea + ea2))

@@ -1,0 +1,219 @@
+from contextlib import ExitStack
+
+import concourse.mybir as mybir
+
+K, T, S, V, N, G, H = 512, 2048, 512, 256, 512, 2048, 512
+FLOPS = 2 * K * H * S + 2 * H * N * V
+
+F32 = mybir.dt.float32
+BF16 = mybir.dt.bfloat16
+I32 = mybir.dt.int32
+U32 = mybir.dt.uint32
+U16 = mybir.dt.uint16
+U8 = mybir.dt.uint8
+FP8X4 = mybir.dt.float8_e4m3fn_x4
+ALU = mybir.AluOpType
+ACT = mybir.ActivationFunctionType
+AX = mybir.AxisListType
+
+P = 128
+PACK = 4
+LIST_COL = 16
+
+
+def tile_picked_hpqhpgateedf_none_p_kernel(
+    tc, x_words, x_scales, d_words, d_scales, gn, w1, tau, tau2, offs, k1, n1, n2, n3, out
+):
+    nc = tc.nc
+    with ExitStack() as ctx:
+        lists = ctx.enter_context(tc.tile_pool(name="lists", bufs=1))
+        keep = ctx.enter_context(tc.tile_pool(name="keep", bufs=1))
+        psum = ctx.enter_context(tc.psum_pool(name="psum", bufs=1))
+
+        k1_t = lists.tile([P, H // LIST_COL], U16, name="k1_t")
+        offs_t = lists.tile([P, S // LIST_COL], U16, name="offs_t")
+        n1_t = lists.tile([P, S // LIST_COL], U16, name="n1_t")
+        n2_t = lists.tile([P, V // LIST_COL], U16, name="n2_t")
+        n3_t = lists.tile([P, V // LIST_COL], U16, name="n3_t")
+
+        d_sc_tab = keep.tile([P, G], U8, name="d_sc_tab", align_bytes=64)
+        x_sc_tab = keep.tile([P, T], U8, name="x_sc_tab", align_bytes=64)
+        d_tab = keep.tile([P, G], U32, name="d_tab", align_bytes=64)
+        x_tab = keep.tile([P, T], U32, name="x_tab", align_bytes=64)
+        planes = keep.tile([P, H + S], U8, name="planes", align_bytes=64)
+        gn_t = keep.tile([P, PACK], F32, name="gn_t")
+        tau_t = keep.tile([P, PACK], F32, name="tau_t")
+        tau2_t = keep.tile([P, PACK], F32, name="tau2_t")
+
+        nc.vector.memset(d_sc_tab[:].bitcast(I32), 0)
+        nc.gpsimd.memset(x_sc_tab[:].bitcast(I32), 0)
+        nc.sync.dma_start(k1_t[:], k1)
+        nc.scalar.dma_start(d_sc_tab[:].bitcast(I32)[0:P:8, :], d_scales[0].bitcast(I32))
+        nc.sync.dma_start(offs_t[:], offs)
+        nc.scalar.dma_start(x_sc_tab[:].bitcast(I32)[0:P:8, :], x_scales[0].bitcast(I32))
+        nc.sync.dma_start(n1_t[:], n1)
+        nc.sync.dma_start(n2_t[:], n2)
+        nc.sync.dma_start(n3_t[:], n3)
+        nc.sync.dma_start(d_tab[:].bitcast(I32), d_words[0].rearrange("p n t -> p (n t)").bitcast(I32))
+        nc.sync.dma_start(x_tab[:].bitcast(I32), x_words[0].rearrange("p n t -> p (n t)").bitcast(I32))
+        nc.gpsimd.dma_start(gn_t[:], gn.rearrange("(p t) o -> p (t o)", t=PACK))
+        nc.gpsimd.dma_start(tau_t[:], tau.rearrange("(p t) o -> p (t o)", t=PACK))
+        nc.gpsimd.dma_start(tau2_t[:], tau2.rearrange("(p t) o -> p (t o)", t=PACK))
+        nc.vector.memset(planes[:].bitcast(I32), 0)
+
+        h2_win = [keep.tile([P, 2 * V], F32, name=f"h2_win{t}", align_bytes=64) for t in range(PACK)]
+        for t in range(PACK):
+            nc.vector.memset(h2_win[t][:, V:], 0.0)
+
+        half_gn = keep.tile([P, PACK], F32, name="half_gn")
+        rates = keep.tile([P, PACK, 2], F32, name="rates")
+        nc.scalar.activation(half_gn[:], gn_t[:], ACT.Copy, scale=0.5)
+        nc.scalar.activation(rates[:, :, 0], tau_t[:], ACT.Copy)
+        nc.scalar.activation(rates[:, :, 1], tau2_t[:], ACT.Copy, scale=-1.0)
+
+        d_sc = keep.tile([P, H], U8, name="d_sc", align_bytes=64)
+        x_sc = keep.tile([P, S], U8, name="x_sc", align_bytes=64)
+        staged = keep.tile([P, H + S], U8, name="staged", tag="staged", align_bytes=64)
+        nc.vector.tensor_copy(d_sc[:], d_sc_tab[:].indirect(k1_t[:]))
+        nc.vector.tensor_copy(x_sc[:], x_sc_tab[:].indirect(offs_t[:]))
+        nc.vector.tensor_copy(
+            staged[:, :H].rearrange("p (t m) -> p t m", t=PACK), d_sc[:].rearrange("p (m t) -> p t m", t=PACK)
+        )
+        nc.vector.tensor_copy(staged[:, H:].bitcast(I32), x_sc[:].bitcast(I32))
+        for q in range(4):
+            nc.scalar.dma_start(
+                planes[:].bitcast(I32)[32 * q : 32 * q + 4, :], staged[:].bitcast(I32)[32 * q : 32 * q + 32 : 8, :]
+            )
+
+        w_raw = keep.tile([P, PACK, N], F32, name="w_raw", tag="staged", align_bytes=64)
+        nc.sync.dma_start(w_raw[:], w1.rearrange("(p j) n -> p j n", j=PACK))
+
+        d_pick = keep.tile([P, H], U32, name="d_pick", align_bytes=64)
+        d_dealt = keep.tile([P, H], U32, name="d_dealt", align_bytes=64)
+        x_pick = keep.tile([P, S], U32, name="x_pick", align_bytes=64)
+        nc.vector.tensor_copy(d_pick[:], d_tab[:].indirect(k1_t[:]))
+        nc.vector.tensor_copy(
+            d_dealt[:].bitcast(I32).rearrange("p (t c i) -> p c t i", t=PACK, i=4),
+            d_pick[:].bitcast(I32).rearrange("p (c i t) -> p c t i", t=PACK, i=4),
+        )
+        HALF = S // 2
+        h_win = [keep.tile([P, S], F32, name=f"h_win{t}", align_bytes=64) for t in range(PACK)]
+        for u in range(2):
+            cols = slice(u * HALF, (u + 1) * HALF)
+            nc.vector.tensor_copy(
+                x_pick[:, cols], x_tab[:].indirect(offs_t[:, u * HALF // LIST_COL : (u + 1) * HALF // LIST_COL])
+            )
+        for t, lo, hi in [(0, 0, HALF), (1, 0, HALF), (0, HALF, S), (1, HALF, S), (2, 0, S), (3, 0, S)]:
+            acc = psum.tile([P, hi - lo], F32, name=f"acc{t}_{lo}", tag=f"bank{t}_{lo}")
+            nc.tensor.matmul_mx(
+                out=acc[:],
+                lhsT=d_dealt[:, t * P : (t + 1) * P].bitcast(FP8X4),
+                lhsT_scale=planes[:, t * P : (t + 1) * P],
+                rhs=x_pick[:, lo:hi].bitcast(FP8X4),
+                rhs_scale=planes[:, H + lo : H + hi],
+                start=True,
+                stop=True,
+            )
+            if hi == HALF:
+                nc.scalar.activation(h_win[t][:, lo:hi], acc[:], ACT.Copy, scale=0.0625)
+            else:
+                nc.vector.tensor_scalar(h_win[t][:, lo:hi], acc[:], 0.0625, None, ALU.mult)
+
+        w_q = keep.tile([P, N], U32, name="w_q", align_bytes=64)
+        w_sc = keep.tile([P, N], U8, name="w_sc", align_bytes=64)
+
+        def round_w(a, copy, tag):
+            w_bf = keep.tile([P, 2, P, PACK], BF16, name=f"w_bf{a}", tag=tag, align_bytes=64)
+            src = w_raw[:].rearrange("p j (c t) -> p c j t", t=PACK)[:, :, :, 2 * a : 2 * a + 2]
+            copy(w_bf[:].rearrange("p t c j -> p c j t"), src)
+            return w_bf
+
+        def quant_w(a, w_bf):
+            nc.vector.quantize_mx(
+                out=w_q[:, 2 * a * P : (2 * a + 2) * P].bitcast(FP8X4),
+                scales=w_sc[:, 2 * a * P : (2 * a + 2) * P],
+                in_=w_bf[:].rearrange("p t c j -> p (t c j)"),
+            )
+
+        z_q = keep.tile([P, V], U32, name="z_q", align_bytes=64)
+        z_sc = keep.tile([P, V], U8, name="z_sc", align_bytes=64)
+        pieces = [(0, 128, [(0, 2), (2, 4)]), (128, 256, [(0, 2), (2, 3), (3, 4)])]
+        for u, (lo, hi, groups) in enumerate(pieces):
+            width = hi - lo
+            ln = keep.tile([P, PACK, width, 2], F32, name=f"ln{u}", align_bytes=64)
+            mx = keep.tile([P, PACK, width], F32, name=f"mx{u}", align_bytes=64)
+            mn = keep.tile([P, PACK, width], F32, name=f"mn{u}", tag=f"mn{u}", align_bytes=64)
+            th = keep.tile([P, PACK, width], F32, name=f"th{u}", tag=f"th{u}", align_bytes=64)
+            y = keep.tile([P, PACK, width], F32, name=f"y{u}", align_bytes=64)
+            z_bf = keep.tile([P, width, PACK], BF16, name=f"z_bf{u}", align_bytes=64)
+            n1_cols = n1_t[:, 2 * lo // LIST_COL : 2 * hi // LIST_COL]
+            for a, b in groups:
+                for t in range(a, b):
+                    nc.scalar.activation(
+                        ln[:, t].rearrange("p v e -> p (v e)"), h_win[t][:].indirect(n1_cols), ACT.Copy
+                    )
+                nc.vector.tensor_tensor(mn[:, a:b], ln[:, a:b, :, 0], ln[:, a:b, :, 1], ALU.min)
+                nc.vector.tensor_tensor(mx[:, a:b], ln[:, a:b, :, 0], ln[:, a:b, :, 1], ALU.max)
+                nc.scalar.activation(th[:, a:b], mn[:, a:b], ACT.Tanh, scale=0.5)
+                nc.vector.scalar_tensor_tensor(y[:, a:b], th[:, a:b], 1.0, mx[:, a:b], ALU.add, ALU.mult)
+            if u == len(pieces) - 1:
+                w_first = round_w(0, nc.scalar.copy, f"mn{u}")
+                w_late = round_w(1, nc.scalar.copy, f"th{u}")
+            nc.vector.tensor_tensor(
+                z_bf[:].rearrange("p (c i) t -> p c t i", i=4),
+                y[:].rearrange("p t (c i) -> p c t i", i=4),
+                half_gn[:].unsqueeze(1).unsqueeze(3).to_broadcast([P, width // 4, PACK, 4]),
+                ALU.mult,
+            )
+            nc.vector.quantize_mx(
+                out=z_q[:, lo:hi].bitcast(FP8X4),
+                scales=z_sc[:, lo:hi],
+                in_=z_bf[:].rearrange("p v t -> p (v t)"),
+            )
+        quant_w(0, w_first)
+
+        out_rows = out.rearrange("(p t) v -> p t v", t=PACK)
+        ends = keep.tile([P, PACK, 2], F32, name="ends")
+        shifts = keep.tile([P, PACK, 2], F32, name="shifts")
+        accs = []
+        for t in range(PACK):
+            if t == 2:
+                quant_w(1, w_late)
+            acc = psum.tile([P, V], F32, name=f"acc2{t}", tag=f"bank{t}_0")
+            accs.append(acc)
+            nc.tensor.matmul_mx(
+                out=acc[:],
+                lhsT=w_q[:, t * P : (t + 1) * P].bitcast(FP8X4),
+                lhsT_scale=w_sc[:, t * P : (t + 1) * P],
+                rhs=z_q[:].bitcast(FP8X4),
+                rhs_scale=z_sc[:],
+                start=True,
+                stop=True,
+            )
+            nc.vector.tensor_scalar(h2_win[t][:, :V], acc[:], 1.0, None, ALU.mult, ALU.max, accum_out=ends[:, t, 0:1])
+            nc.vector.tensor_reduce(ends[:, t, 1:2], acc[:], AX.X, ALU.min)
+            for e0, e1 in [(0, 1), (1, 2)] if t == 0 else [(0, 2)]:
+                nc.vector.scalar_tensor_tensor(
+                    shifts[:, t, e0:e1], ends[:, t, e0:e1], -1.0, rates[:, t, e0:e1], ALU.mult, ALU.mult
+                )
+        for t in range(PACK):
+            ea = keep.tile([P, V], F32, name=f"ea{t}")
+            eb = keep.tile([P, V], F32, name=f"eb{t}")
+            both = keep.tile([P, V], F32, name=f"both{t}")
+            res = keep.tile([P, V], F32, name=f"res{t}")
+            parts = 2 if t == PACK - 1 else 1
+            width = V // parts
+            for s in range(parts):
+                cols = slice(s * width, (s + 1) * width)
+                lcols = slice(s * width // LIST_COL, (s + 1) * width // LIST_COL)
+                nc.scalar.activation(
+                    ea[:, cols], h2_win[t][:].indirect(n2_t[:, lcols]), ACT.Exp,
+                    bias=shifts[:, t, 0:1], scale=rates[:, t, 0:1],
+                )
+                nc.scalar.activation(
+                    eb[:, cols], h2_win[t][:].indirect(n3_t[:, lcols]), ACT.Exp,
+                    bias=shifts[:, t, 1:2], scale=rates[:, t, 1:2],
+                )
+                (nc.vector if t == PACK - 1 else nc.gpsimd).tensor_tensor(both[:, cols], ea[:, cols], eb[:, cols], ALU.add)
+                nc.vector.scalar_tensor_tensor(res[:, cols], both[:, cols], 1.5, accs[t][:, cols], ALU.mult, ALU.mult)
+                nc.sync.dma_start(out_rows[:, t, cols], res[:, cols])

@@ -45,12 +45,12 @@ def tile_picked_hpqhpgateedf_none_p_kernel(
         tau_t = keep.tile([P, PACK], F32, name="tau_t")
         tau2_t = keep.tile([P, PACK], F32, name="tau2_t")
 
-        nc.vector.memset(d_sc_tab[:].bitcast(I32), 0)
-        nc.gpsimd.memset(x_sc_tab[:].bitcast(I32), 0)
+        nc.gpsimd.memset(d_sc_tab[:].bitcast(I32), 0)
+        nc.vector.memset(x_sc_tab[:].bitcast(I32), 0)
         nc.sync.dma_start(k1_t[:], k1)
-        nc.scalar.dma_start(d_sc_tab[:].bitcast(I32)[0:P:8, :], d_scales[0].bitcast(I32))
+        nc.sync.dma_start(d_sc_tab[:].bitcast(I32)[0:P:8, :], d_scales[0].bitcast(I32))
         nc.sync.dma_start(offs_t[:], offs)
-        nc.scalar.dma_start(x_sc_tab[:].bitcast(I32)[0:P:8, :], x_scales[0].bitcast(I32))
+        nc.sync.dma_start(x_sc_tab[:].bitcast(I32)[0:P:8, :], x_scales[0].bitcast(I32))
         nc.sync.dma_start(n1_t[:], n1)
         nc.sync.dma_start(n2_t[:], n2)
         nc.sync.dma_start(n3_t[:], n3)
@@ -67,12 +67,12 @@ def tile_picked_hpqhpgateedf_none_p_kernel(
 
         half_gn = keep.tile([P, PACK], F32, name="half_gn")
         rates = keep.tile([P, PACK, 2], F32, name="rates")
-        nc.scalar.activation(half_gn[:], gn_t[:], ACT.Copy, scale=0.5)
-        nc.scalar.activation(rates[:, :, 0], tau_t[:], ACT.Copy)
-        nc.scalar.activation(rates[:, :, 1], tau2_t[:], ACT.Copy, scale=-1.0)
+        nc.gpsimd.tensor_scalar(half_gn[:], gn_t[:], 0.5, 0.0, ALU.mult, ALU.add)
+        nc.gpsimd.tensor_copy(rates[:, :, 0], tau_t[:])
+        nc.gpsimd.tensor_scalar(rates[:, :, 1], tau2_t[:], -1.0, 0.0, ALU.mult, ALU.add)
 
         d_sc = keep.tile([P, H], U8, name="d_sc", align_bytes=64)
-        x_sc = keep.tile([P, S], U8, name="x_sc", align_bytes=64)
+        x_sc = keep.tile([P, S], U8, name="x_sc", tag="x_sc", align_bytes=64)
         staged = keep.tile([P, H + S], U8, name="staged", tag="staged", align_bytes=64)
         nc.vector.tensor_copy(d_sc[:], d_sc_tab[:].indirect(k1_t[:]))
         nc.vector.tensor_copy(x_sc[:], x_sc_tab[:].indirect(offs_t[:]))
@@ -81,14 +81,11 @@ def tile_picked_hpqhpgateedf_none_p_kernel(
         )
         nc.vector.tensor_copy(staged[:, H:].bitcast(I32), x_sc[:].bitcast(I32))
         for q in range(4):
-            nc.scalar.dma_start(
+            (nc.scalar if q % 2 else nc.sync).dma_start(
                 planes[:].bitcast(I32)[32 * q : 32 * q + 4, :], staged[:].bitcast(I32)[32 * q : 32 * q + 32 : 8, :]
             )
 
-        w_raw = keep.tile([P, PACK, N], F32, name="w_raw", tag="staged", align_bytes=64)
-        nc.sync.dma_start(w_raw[:], w1.rearrange("(p j) n -> p j n", j=PACK))
-
-        d_pick = keep.tile([P, H], U32, name="d_pick", align_bytes=64)
+        d_pick = keep.tile([P, H], U32, name="d_pick", tag="x_sc", align_bytes=64)
         d_dealt = keep.tile([P, H], U32, name="d_dealt", align_bytes=64)
         x_pick = keep.tile([P, S], U32, name="x_pick", align_bytes=64)
         nc.vector.tensor_copy(d_pick[:], d_tab[:].indirect(k1_t[:]))
@@ -96,6 +93,8 @@ def tile_picked_hpqhpgateedf_none_p_kernel(
             d_dealt[:].bitcast(I32).rearrange("p (t c i) -> p c t i", t=PACK, i=4),
             d_pick[:].bitcast(I32).rearrange("p (c i t) -> p c t i", t=PACK, i=4),
         )
+        w_raw = keep.tile([P, PACK, N], F32, name="w_raw", tag="x_sc", align_bytes=64)
+        nc.sync.dma_start(w_raw[:], w1.rearrange("(p j) n -> p j n", j=PACK))
         HALF = S // 2
         h_win = [keep.tile([P, S], F32, name=f"h_win{t}", align_bytes=64) for t in range(PACK)]
         for u in range(2):
@@ -137,40 +136,58 @@ def tile_picked_hpqhpgateedf_none_p_kernel(
 
         z_q = keep.tile([P, V], U32, name="z_q", align_bytes=64)
         z_sc = keep.tile([P, V], U8, name="z_sc", align_bytes=64)
-        pieces = [(0, 128, [(0, 2), (2, 4)]), (128, 256, [(0, 2), (2, 3), (3, 4)])]
-        for u, (lo, hi, groups) in enumerate(pieces):
-            width = hi - lo
-            ln = keep.tile([P, PACK, width, 2], F32, name=f"ln{u}", align_bytes=64)
-            mx = keep.tile([P, PACK, width], F32, name=f"mx{u}", align_bytes=64)
-            mn = keep.tile([P, PACK, width], F32, name=f"mn{u}", tag=f"mn{u}", align_bytes=64)
-            th = keep.tile([P, PACK, width], F32, name=f"th{u}", tag=f"th{u}", align_bytes=64)
-            y = keep.tile([P, PACK, width], F32, name=f"y{u}", align_bytes=64)
-            z_bf = keep.tile([P, width, PACK], BF16, name=f"z_bf{u}", align_bytes=64)
-            n1_cols = n1_t[:, 2 * lo // LIST_COL : 2 * hi // LIST_COL]
-            for a, b in groups:
+        VH = V // 2
+        for u in range(2):
+            ln = [
+                keep.tile([P, 2, VH, 2], F32, name=f"ln{u}_{pair}", tag=f"ln{pair}", align_bytes=64)
+                for pair in range(2)
+            ]
+            mx = keep.tile([P, PACK, VH], F32, name=f"mx{u}", align_bytes=64)
+            mn = keep.tile([P, PACK, VH], F32, name=f"mn{u}", tag=f"mn{u}", align_bytes=64)
+            th = keep.tile([P, PACK, VH], F32, name=f"th{u}", align_bytes=64)
+            y = keep.tile([P, PACK, VH], F32, name=f"y{u}", align_bytes=64)
+            z_bf = keep.tile([P, VH, PACK], BF16, name=f"z_bf{u}", align_bytes=64)
+
+            def gate(a, b, lo, hi):
+                first = 2 * (u * VH + lo) // LIST_COL
+                n1_cols = n1_t[:, first : first + 2 * (hi - lo) // LIST_COL]
                 for t in range(a, b):
                     nc.scalar.activation(
-                        ln[:, t].rearrange("p v e -> p (v e)"), h_win[t][:].indirect(n1_cols), ACT.Copy
+                        ln[t // 2][:, t % 2, lo:hi].rearrange("p v e -> p (v e)"), h_win[t][:].indirect(n1_cols), ACT.Copy
                     )
-                nc.vector.tensor_tensor(mn[:, a:b], ln[:, a:b, :, 0], ln[:, a:b, :, 1], ALU.min)
-                nc.vector.tensor_tensor(mx[:, a:b], ln[:, a:b, :, 0], ln[:, a:b, :, 1], ALU.max)
-                nc.scalar.activation(th[:, a:b], mn[:, a:b], ACT.Tanh, scale=0.5)
-                nc.vector.scalar_tensor_tensor(y[:, a:b], th[:, a:b], 1.0, mx[:, a:b], ALU.add, ALU.mult)
-            if u == len(pieces) - 1:
-                w_first = round_w(0, nc.scalar.copy, f"mn{u}")
-                w_late = round_w(1, nc.scalar.copy, f"th{u}")
-            nc.vector.tensor_tensor(
-                z_bf[:].rearrange("p (c i) t -> p c t i", i=4),
-                y[:].rearrange("p t (c i) -> p c t i", i=4),
-                half_gn[:].unsqueeze(1).unsqueeze(3).to_broadcast([P, width // 4, PACK, 4]),
-                ALU.mult,
-            )
-            nc.vector.quantize_mx(
-                out=z_q[:, lo:hi].bitcast(FP8X4),
-                scales=z_sc[:, lo:hi],
-                in_=z_bf[:].rearrange("p v t -> p (v t)"),
-            )
-        quant_w(0, w_first)
+                pairs = ln[a // 2][:, a % 2 : a % 2 + b - a, lo:hi]
+                nc.vector.tensor_tensor(mn[:, a:b, lo:hi], pairs[:, :, :, 0], pairs[:, :, :, 1], ALU.min)
+                nc.vector.tensor_tensor(mx[:, a:b, lo:hi], pairs[:, :, :, 0], pairs[:, :, :, 1], ALU.max)
+                nc.scalar.activation(th[:, a:b, lo:hi], mn[:, a:b, lo:hi], ACT.Tanh, scale=0.5)
+                for t in range(a, b):
+                    g = half_gn[:, t : t + 1]
+                    nc.vector.tensor_scalar(y[:, t, lo:hi], th[:, t, lo:hi], g, g, ALU.mult, ALU.add)
+
+            def quant_z(lo, hi):
+                nc.vector.tensor_tensor(
+                    z_bf[:, lo:hi].rearrange("p (c i) t -> p c t i", i=4),
+                    y[:, :, lo:hi].rearrange("p t (c i) -> p c t i", i=4),
+                    mx[:, :, lo:hi].rearrange("p t (c i) -> p c t i", i=4),
+                    ALU.mult,
+                )
+                nc.vector.quantize_mx(
+                    out=z_q[:, u * VH + lo : u * VH + hi].bitcast(FP8X4),
+                    scales=z_sc[:, u * VH + lo : u * VH + hi],
+                    in_=z_bf[:, lo:hi].rearrange("p v t -> p (v t)"),
+                )
+
+            gate(0, 2, 0, VH)
+            if u == 0:
+                gate(2, 4, 0, VH)
+                quant_z(0, VH)
+                quant_w(0, round_w(0, nc.vector.tensor_copy, "w_first"))
+            else:
+                gate(2, 3, 0, VH)
+                gate(3, 4, 0, VH // 2)
+                quant_z(0, VH // 2)
+                gate(3, 4, VH // 2, VH)
+                w_late = round_w(1, nc.scalar.copy, "mn1")
+                quant_z(VH // 2, VH)
 
         out_rows = out.rearrange("(p t) v -> p t v", t=PACK)
         ends = keep.tile([P, PACK, 2], F32, name="ends")
@@ -214,6 +231,6 @@ def tile_picked_hpqhpgateedf_none_p_kernel(
                     eb[:, cols], h2_win[t][:].indirect(n3_t[:, lcols]), ACT.Exp,
                     bias=shifts[:, t, 1:2], scale=rates[:, t, 1:2],
                 )
-                (nc.vector if t == PACK - 1 else nc.gpsimd).tensor_tensor(both[:, cols], ea[:, cols], eb[:, cols], ALU.add)
+                nc.vector.tensor_tensor(both[:, cols], ea[:, cols], eb[:, cols], ALU.add)
                 nc.vector.scalar_tensor_tensor(res[:, cols], both[:, cols], 1.5, accs[t][:, cols], ALU.mult, ALU.mult)
                 nc.sync.dma_start(out_rows[:, t, cols], res[:, cols])

@@ -45,12 +45,12 @@ def tile_picked_hpqhpgateedf_none_p_kernel(
         tau_t = keep.tile([P, PACK], F32, name="tau_t")
         tau2_t = keep.tile([P, PACK], F32, name="tau2_t")
 
-        nc.gpsimd.memset(d_sc_tab[:].bitcast(I32), 0)
         nc.vector.memset(x_sc_tab[:].bitcast(I32), 0)
-        nc.sync.dma_start(k1_t[:], k1)
-        nc.sync.dma_start(d_sc_tab[:].bitcast(I32)[0:P:8, :], d_scales[0].bitcast(I32))
+        nc.vector.memset(d_sc_tab[:].bitcast(I32), 0)
         nc.sync.dma_start(offs_t[:], offs)
         nc.sync.dma_start(x_sc_tab[:].bitcast(I32)[0:P:8, :], x_scales[0].bitcast(I32))
+        nc.sync.dma_start(k1_t[:], k1)
+        nc.sync.dma_start(d_sc_tab[:].bitcast(I32)[0:P:8, :], d_scales[0].bitcast(I32))
         nc.sync.dma_start(n1_t[:], n1)
         nc.sync.dma_start(n2_t[:], n2)
         nc.sync.dma_start(n3_t[:], n3)
@@ -70,18 +70,20 @@ def tile_picked_hpqhpgateedf_none_p_kernel(
         nc.gpsimd.tensor_scalar(half_gn[:], gn_t[:], 0.5, 0.0, ALU.mult, ALU.add)
         nc.gpsimd.tensor_copy(rates[:, :, 0], tau_t[:])
         nc.gpsimd.tensor_scalar(rates[:, :, 1], tau2_t[:], -1.0, 0.0, ALU.mult, ALU.add)
+        minus_rates = keep.tile([P, PACK, 2], F32, name="minus_rates")
+        nc.gpsimd.tensor_scalar(minus_rates[:], rates[:], -1.0, 0.0, ALU.mult, ALU.add)
 
-        d_sc = keep.tile([P, H], U8, name="d_sc", align_bytes=64)
+        d_sc = keep.tile([P, H], U8, name="d_sc", tag="d_sc", align_bytes=64)
         x_sc = keep.tile([P, S], U8, name="x_sc", tag="x_sc", align_bytes=64)
         staged = keep.tile([P, H + S], U8, name="staged", tag="staged", align_bytes=64)
-        nc.vector.tensor_copy(d_sc[:], d_sc_tab[:].indirect(k1_t[:]))
         nc.vector.tensor_copy(x_sc[:], x_sc_tab[:].indirect(offs_t[:]))
+        nc.vector.tensor_copy(d_sc[:], d_sc_tab[:].indirect(k1_t[:]))
+        nc.vector.tensor_copy(staged[:, H:].bitcast(I32), x_sc[:].bitcast(I32))
         nc.vector.tensor_copy(
             staged[:, :H].rearrange("p (t m) -> p t m", t=PACK), d_sc[:].rearrange("p (m t) -> p t m", t=PACK)
         )
-        nc.vector.tensor_copy(staged[:, H:].bitcast(I32), x_sc[:].bitcast(I32))
         for q in range(4):
-            (nc.scalar if q % 2 else nc.sync).dma_start(
+            nc.sync.dma_start(
                 planes[:].bitcast(I32)[32 * q : 32 * q + 4, :], staged[:].bitcast(I32)[32 * q : 32 * q + 32 : 8, :]
             )
 
@@ -93,7 +95,7 @@ def tile_picked_hpqhpgateedf_none_p_kernel(
             d_dealt[:].bitcast(I32).rearrange("p (t c i) -> p c t i", t=PACK, i=4),
             d_pick[:].bitcast(I32).rearrange("p (c i t) -> p c t i", t=PACK, i=4),
         )
-        w_raw = keep.tile([P, PACK, N], F32, name="w_raw", tag="x_sc", align_bytes=64)
+        w_raw = keep.tile([P, PACK, N], F32, name="w_raw", tag="d_sc", align_bytes=64)
         nc.sync.dma_start(w_raw[:], w1.rearrange("(p j) n -> p j n", j=PACK))
         HALF = S // 2
         h_win = [keep.tile([P, S], F32, name=f"h_win{t}", align_bytes=64) for t in range(PACK)]
@@ -136,14 +138,28 @@ def tile_picked_hpqhpgateedf_none_p_kernel(
 
         z_q = keep.tile([P, V], U32, name="z_q", align_bytes=64)
         z_sc = keep.tile([P, V], U8, name="z_sc", align_bytes=64)
+        def product2(t, lo, hi, bank, ends):
+            acc = psum.tile([P, hi - lo], F32, name=f"acc2_{t}_{lo}", tag=bank)
+            nc.tensor.matmul_mx(
+                out=acc[:],
+                lhsT=w_q[:, t * P : (t + 1) * P].bitcast(FP8X4),
+                lhsT_scale=w_sc[:, t * P : (t + 1) * P],
+                rhs=z_q[:, lo:hi].bitcast(FP8X4),
+                rhs_scale=z_sc[:, lo:hi],
+                start=True,
+                stop=True,
+            )
+            nc.vector.tensor_scalar(h2_win[t][:, lo:hi], acc[:], 1.0, None, ALU.mult, ALU.max, accum_out=ends[:, 0:1])
+            nc.vector.tensor_reduce(ends[:, 1:2], acc[:], AX.X, ALU.min)
+
         VH = V // 2
+        ends_early = keep.tile([P, 2], F32, name="ends_early")
         for u in range(2):
             ln = [
                 keep.tile([P, 2, VH, 2], F32, name=f"ln{u}_{pair}", tag=f"ln{pair}", align_bytes=64)
                 for pair in range(2)
             ]
             mx = keep.tile([P, PACK, VH], F32, name=f"mx{u}", align_bytes=64)
-            mn = keep.tile([P, PACK, VH], F32, name=f"mn{u}", tag=f"mn{u}", align_bytes=64)
             th = keep.tile([P, PACK, VH], F32, name=f"th{u}", align_bytes=64)
             y = keep.tile([P, PACK, VH], F32, name=f"y{u}", align_bytes=64)
             z_bf = keep.tile([P, VH, PACK], BF16, name=f"z_bf{u}", align_bytes=64)
@@ -156,9 +172,10 @@ def tile_picked_hpqhpgateedf_none_p_kernel(
                         ln[t // 2][:, t % 2, lo:hi].rearrange("p v e -> p (v e)"), h_win[t][:].indirect(n1_cols), ACT.Copy
                     )
                 pairs = ln[a // 2][:, a % 2 : a % 2 + b - a, lo:hi]
-                nc.vector.tensor_tensor(mn[:, a:b, lo:hi], pairs[:, :, :, 0], pairs[:, :, :, 1], ALU.min)
+                mn = small[a // 2][:, a % 2 : a % 2 + b - a, lo:hi]
+                nc.vector.tensor_tensor(mn, pairs[:, :, :, 0], pairs[:, :, :, 1], ALU.min)
                 nc.vector.tensor_tensor(mx[:, a:b, lo:hi], pairs[:, :, :, 0], pairs[:, :, :, 1], ALU.max)
-                nc.scalar.activation(th[:, a:b, lo:hi], mn[:, a:b, lo:hi], ACT.Tanh, scale=0.5)
+                nc.scalar.activation(th[:, a:b, lo:hi], mn, ACT.Tanh, scale=0.5)
                 for t in range(a, b):
                     g = half_gn[:, t : t + 1]
                     nc.vector.tensor_scalar(y[:, t, lo:hi], th[:, t, lo:hi], g, g, ALU.mult, ALU.add)
@@ -176,43 +193,36 @@ def tile_picked_hpqhpgateedf_none_p_kernel(
                     in_=z_bf[:, lo:hi].rearrange("p v t -> p (v t)"),
                 )
 
+            small = [keep.tile([P, 2, VH], F32, name=f"mn{u}_0", align_bytes=64)]
             gate(0, 2, 0, VH)
+            if u == 0:
+                quant_w(0, round_w(0, nc.vector.tensor_copy, "shared0"))
+            small.append(keep.tile([P, 2, VH], F32, name=f"mn{u}_1", tag=f"shared{u}", align_bytes=64))
             if u == 0:
                 gate(2, 4, 0, VH)
                 quant_z(0, VH)
-                quant_w(0, round_w(0, nc.vector.tensor_copy, "w_first"))
+                product2(0, 0, VH, "bank0_0", ends_early[:])
             else:
                 gate(2, 3, 0, VH)
                 gate(3, 4, 0, VH // 2)
                 quant_z(0, VH // 2)
                 gate(3, 4, VH // 2, VH)
-                w_late = round_w(1, nc.scalar.copy, "mn1")
+                w_late = round_w(1, nc.scalar.copy, "shared1")
                 quant_z(VH // 2, VH)
 
         out_rows = out.rearrange("(p t) v -> p t v", t=PACK)
         ends = keep.tile([P, PACK, 2], F32, name="ends")
         shifts = keep.tile([P, PACK, 2], F32, name="shifts")
-        accs = []
-        for t in range(PACK):
+        product2(0, VH, V, f"bank0_{HALF}", ends[:, 0])
+        for e, op in enumerate([ALU.max, ALU.min]):
+            nc.vector.scalar_tensor_tensor(
+                shifts[:, 0, e : e + 1], ends[:, 0, e : e + 1], ends_early[:, e : e + 1], minus_rates[:, 0, e : e + 1], op, ALU.mult
+            )
+        for t in range(1, PACK):
             if t == 2:
                 quant_w(1, w_late)
-            acc = psum.tile([P, V], F32, name=f"acc2{t}", tag=f"bank{t}_0")
-            accs.append(acc)
-            nc.tensor.matmul_mx(
-                out=acc[:],
-                lhsT=w_q[:, t * P : (t + 1) * P].bitcast(FP8X4),
-                lhsT_scale=w_sc[:, t * P : (t + 1) * P],
-                rhs=z_q[:].bitcast(FP8X4),
-                rhs_scale=z_sc[:],
-                start=True,
-                stop=True,
-            )
-            nc.vector.tensor_scalar(h2_win[t][:, :V], acc[:], 1.0, None, ALU.mult, ALU.max, accum_out=ends[:, t, 0:1])
-            nc.vector.tensor_reduce(ends[:, t, 1:2], acc[:], AX.X, ALU.min)
-            for e0, e1 in [(0, 1), (1, 2)] if t == 0 else [(0, 2)]:
-                nc.vector.scalar_tensor_tensor(
-                    shifts[:, t, e0:e1], ends[:, t, e0:e1], -1.0, rates[:, t, e0:e1], ALU.mult, ALU.mult
-                )
+            product2(t, 0, V, f"bank{t}_0", ends[:, t])
+            nc.vector.tensor_tensor(shifts[:, t], ends[:, t], minus_rates[:, t], ALU.mult)
         for t in range(PACK):
             ea = keep.tile([P, V], F32, name=f"ea{t}")
             eb = keep.tile([P, V], F32, name=f"eb{t}")
@@ -232,5 +242,5 @@ def tile_picked_hpqhpgateedf_none_p_kernel(
                     bias=shifts[:, t, 1:2], scale=rates[:, t, 1:2],
                 )
                 nc.vector.tensor_tensor(both[:, cols], ea[:, cols], eb[:, cols], ALU.add)
-                nc.vector.scalar_tensor_tensor(res[:, cols], both[:, cols], 1.5, accs[t][:, cols], ALU.mult, ALU.mult)
+                nc.vector.scalar_tensor_tensor(res[:, cols], both[:, cols], 1.5, h2_win[t][:, cols], ALU.mult, ALU.mult)
                 nc.sync.dma_start(out_rows[:, t, cols], res[:, cols])

@@ -19,6 +19,11 @@ AX = mybir.AxisListType
 P = 128
 PACK = 4
 LIST_COL = 16
+BLOCK_PARTS = 8
+QUAD = 32
+LINE = 4
+SH = S // 2
+VH = V // 2
 
 
 def tile_picked_hpqhpgateedf_none_p_kernel(
@@ -48,14 +53,14 @@ def tile_picked_hpqhpgateedf_none_p_kernel(
         nc.vector.memset(x_sc_tab[:].bitcast(I32), 0)
         nc.vector.memset(d_sc_tab[:].bitcast(I32), 0)
         nc.sync.dma_start(offs_t[:], offs)
-        nc.sync.dma_start(x_sc_tab[:].bitcast(I32)[0:P:8, :], x_scales[0].bitcast(I32))
+        nc.sync.dma_start(x_sc_tab[:].bitcast(I32)[0:P:BLOCK_PARTS, :], x_scales[0].bitcast(I32))
         nc.sync.dma_start(k1_t[:], k1)
-        nc.sync.dma_start(d_sc_tab[:].bitcast(I32)[0:P:8, :], d_scales[0].bitcast(I32))
+        nc.sync.dma_start(d_sc_tab[:].bitcast(I32)[0:P:BLOCK_PARTS, :], d_scales[0].bitcast(I32))
         nc.sync.dma_start(n1_t[:], n1)
         nc.sync.dma_start(n2_t[:], n2)
-        nc.sync.dma_start(n3_t[:], n3)
         nc.sync.dma_start(d_tab[:].bitcast(I32), d_words[0].rearrange("p n t -> p (n t)").bitcast(I32))
         nc.sync.dma_start(x_tab[:].bitcast(I32), x_words[0].rearrange("p n t -> p (n t)").bitcast(I32))
+        nc.sync.dma_start(n3_t[:], n3)
         nc.gpsimd.dma_start(gn_t[:], gn.rearrange("(p t) o -> p (t o)", t=PACK))
         nc.gpsimd.dma_start(tau_t[:], tau.rearrange("(p t) o -> p (t o)", t=PACK))
         nc.gpsimd.dma_start(tau2_t[:], tau2.rearrange("(p t) o -> p (t o)", t=PACK))
@@ -75,16 +80,17 @@ def tile_picked_hpqhpgateedf_none_p_kernel(
 
         d_sc = keep.tile([P, H], U8, name="d_sc", tag="d_sc", align_bytes=64)
         x_sc = keep.tile([P, S], U8, name="x_sc", tag="x_sc", align_bytes=64)
-        staged = keep.tile([P, H + S], U8, name="staged", tag="staged", align_bytes=64)
+        staged = keep.tile([P, H + S], U8, name="staged", align_bytes=64)
         nc.vector.tensor_copy(x_sc[:], x_sc_tab[:].indirect(offs_t[:]))
         nc.vector.tensor_copy(d_sc[:], d_sc_tab[:].indirect(k1_t[:]))
         nc.vector.tensor_copy(staged[:, H:].bitcast(I32), x_sc[:].bitcast(I32))
         nc.vector.tensor_copy(
             staged[:, :H].rearrange("p (t m) -> p t m", t=PACK), d_sc[:].rearrange("p (m t) -> p t m", t=PACK)
         )
-        for q in range(4):
+        for q0 in range(0, P, QUAD):
             nc.sync.dma_start(
-                planes[:].bitcast(I32)[32 * q : 32 * q + 4, :], staged[:].bitcast(I32)[32 * q : 32 * q + 32 : 8, :]
+                planes[:].bitcast(I32)[q0 : q0 + QUAD // BLOCK_PARTS, :],
+                staged[:].bitcast(I32)[q0 : q0 + QUAD : BLOCK_PARTS, :],
             )
 
         d_pick = keep.tile([P, H], U32, name="d_pick", tag="x_sc", align_bytes=64)
@@ -92,19 +98,21 @@ def tile_picked_hpqhpgateedf_none_p_kernel(
         x_pick = keep.tile([P, S], U32, name="x_pick", align_bytes=64)
         nc.vector.tensor_copy(d_pick[:], d_tab[:].indirect(k1_t[:]))
         nc.vector.tensor_copy(
-            d_dealt[:].bitcast(I32).rearrange("p (t c i) -> p c t i", t=PACK, i=4),
-            d_pick[:].bitcast(I32).rearrange("p (c i t) -> p c t i", t=PACK, i=4),
+            d_dealt[:].bitcast(I32).rearrange("p (t c i) -> p c t i", t=PACK, i=LINE),
+            d_pick[:].bitcast(I32).rearrange("p (c i t) -> p c t i", t=PACK, i=LINE),
         )
         w_raw = keep.tile([P, PACK, N], F32, name="w_raw", tag="d_sc", align_bytes=64)
         nc.sync.dma_start(w_raw[:], w1.rearrange("(p j) n -> p j n", j=PACK))
-        HALF = S // 2
         h_win = [keep.tile([P, S], F32, name=f"h_win{t}", align_bytes=64) for t in range(PACK)]
-        for u in range(2):
-            cols = slice(u * HALF, (u + 1) * HALF)
+        for lo in range(0, S, SH):
             nc.vector.tensor_copy(
-                x_pick[:, cols], x_tab[:].indirect(offs_t[:, u * HALF // LIST_COL : (u + 1) * HALF // LIST_COL])
+                x_pick[:, lo : lo + SH], x_tab[:].indirect(offs_t[:, lo // LIST_COL : (lo + SH) // LIST_COL])
             )
-        for t, lo, hi in [(0, 0, HALF), (1, 0, HALF), (0, HALF, S), (1, HALF, S), (2, 0, S), (3, 0, S)]:
+
+        first_halves = [(t, 0, SH) for t in range(2)]
+        second_halves = [(t, SH, S) for t in range(2)]
+        whole_rows = [(t, 0, S) for t in range(2, PACK)]
+        for t, lo, hi in first_halves + second_halves + whole_rows:
             acc = psum.tile([P, hi - lo], F32, name=f"acc{t}_{lo}", tag=f"bank{t}_{lo}")
             nc.tensor.matmul_mx(
                 out=acc[:],
@@ -115,7 +123,7 @@ def tile_picked_hpqhpgateedf_none_p_kernel(
                 start=True,
                 stop=True,
             )
-            if hi == HALF:
+            if hi == SH:
                 nc.scalar.activation(h_win[t][:, lo:hi], acc[:], ACT.Copy, scale=0.0625)
             else:
                 nc.vector.tensor_scalar(h_win[t][:, lo:hi], acc[:], 0.0625, None, ALU.mult)
@@ -138,10 +146,11 @@ def tile_picked_hpqhpgateedf_none_p_kernel(
 
         z_q = keep.tile([P, V], U32, name="z_q", align_bytes=64)
         z_sc = keep.tile([P, V], U8, name="z_sc", align_bytes=64)
-        def product2(t, lo, hi, bank, ends):
-            acc = psum.tile([P, hi - lo], F32, name=f"acc2_{t}_{lo}", tag=bank)
+
+        def second_product(t, lo, hi, bank, top_low):
+            acc2 = psum.tile([P, hi - lo], F32, name=f"acc2_{t}_{lo}", tag=bank)
             nc.tensor.matmul_mx(
-                out=acc[:],
+                out=acc2[:],
                 lhsT=w_q[:, t * P : (t + 1) * P].bitcast(FP8X4),
                 lhsT_scale=w_sc[:, t * P : (t + 1) * P],
                 rhs=z_q[:, lo:hi].bitcast(FP8X4),
@@ -149,42 +158,44 @@ def tile_picked_hpqhpgateedf_none_p_kernel(
                 start=True,
                 stop=True,
             )
-            nc.vector.tensor_scalar(h2_win[t][:, lo:hi], acc[:], 1.0, None, ALU.mult, ALU.max, accum_out=ends[:, 0:1])
-            nc.vector.tensor_reduce(ends[:, 1:2], acc[:], AX.X, ALU.min)
+            nc.vector.tensor_scalar(
+                h2_win[t][:, lo:hi], acc2[:], 1.0, None, ALU.mult, ALU.max, accum_out=top_low[:, 0:1]
+            )
+            nc.vector.tensor_reduce(top_low[:, 1:2], acc2[:], AX.X, ALU.min)
 
-        VH = V // 2
         ends_early = keep.tile([P, 2], F32, name="ends_early")
         for u in range(2):
             ln = [
-                keep.tile([P, 2, VH, 2], F32, name=f"ln{u}_{pair}", tag=f"ln{pair}", align_bytes=64)
-                for pair in range(2)
+                keep.tile([P, 2, VH, 2], F32, name=f"ln{u}_{two}", tag=f"ln{two}", align_bytes=64) for two in range(2)
             ]
             mx = keep.tile([P, PACK, VH], F32, name=f"mx{u}", align_bytes=64)
             th = keep.tile([P, PACK, VH], F32, name=f"th{u}", align_bytes=64)
-            y = keep.tile([P, PACK, VH], F32, name=f"y{u}", align_bytes=64)
+            gate = keep.tile([P, PACK, VH], F32, name=f"gate{u}", align_bytes=64)
             z_bf = keep.tile([P, VH, PACK], BF16, name=f"z_bf{u}", align_bytes=64)
 
-            def gate(a, b, lo, hi):
+            def pool_pairs(a, b, lo, hi):
                 first = 2 * (u * VH + lo) // LIST_COL
                 n1_cols = n1_t[:, first : first + 2 * (hi - lo) // LIST_COL]
                 for t in range(a, b):
                     nc.scalar.activation(
-                        ln[t // 2][:, t % 2, lo:hi].rearrange("p v e -> p (v e)"), h_win[t][:].indirect(n1_cols), ACT.Copy
+                        ln[t // 2][:, t % 2, lo:hi].rearrange("p v e -> p (v e)"),
+                        h_win[t][:].indirect(n1_cols),
+                        ACT.Copy,
                     )
                 pairs = ln[a // 2][:, a % 2 : a % 2 + b - a, lo:hi]
-                mn = small[a // 2][:, a % 2 : a % 2 + b - a, lo:hi]
-                nc.vector.tensor_tensor(mn, pairs[:, :, :, 0], pairs[:, :, :, 1], ALU.min)
+                smaller = mn[a // 2][:, a % 2 : a % 2 + b - a, lo:hi]
+                nc.vector.tensor_tensor(smaller, pairs[:, :, :, 0], pairs[:, :, :, 1], ALU.min)
                 nc.vector.tensor_tensor(mx[:, a:b, lo:hi], pairs[:, :, :, 0], pairs[:, :, :, 1], ALU.max)
-                nc.scalar.activation(th[:, a:b, lo:hi], mn, ACT.Tanh, scale=0.5)
+                nc.scalar.activation(th[:, a:b, lo:hi], smaller, ACT.Tanh, scale=0.5)
                 for t in range(a, b):
                     g = half_gn[:, t : t + 1]
-                    nc.vector.tensor_scalar(y[:, t, lo:hi], th[:, t, lo:hi], g, g, ALU.mult, ALU.add)
+                    nc.vector.tensor_scalar(gate[:, t, lo:hi], th[:, t, lo:hi], g, g, ALU.mult, ALU.add)
 
             def quant_z(lo, hi):
                 nc.vector.tensor_tensor(
-                    z_bf[:, lo:hi].rearrange("p (c i) t -> p c t i", i=4),
-                    y[:, :, lo:hi].rearrange("p t (c i) -> p c t i", i=4),
-                    mx[:, :, lo:hi].rearrange("p t (c i) -> p c t i", i=4),
+                    z_bf[:, lo:hi].rearrange("p (c i) t -> p c t i", i=LINE),
+                    gate[:, :, lo:hi].rearrange("p t (c i) -> p c t i", i=LINE),
+                    mx[:, :, lo:hi].rearrange("p t (c i) -> p c t i", i=LINE),
                     ALU.mult,
                 )
                 nc.vector.quantize_mx(
@@ -193,54 +204,67 @@ def tile_picked_hpqhpgateedf_none_p_kernel(
                     in_=z_bf[:, lo:hi].rearrange("p v t -> p (v t)"),
                 )
 
-            small = [keep.tile([P, 2, VH], F32, name=f"mn{u}_0", align_bytes=64)]
-            gate(0, 2, 0, VH)
+            mn = [keep.tile([P, 2, VH], F32, name=f"mn{u}_0", align_bytes=64)]
+            pool_pairs(0, 2, 0, VH)
             if u == 0:
                 quant_w(0, round_w(0, nc.vector.tensor_copy, "shared0"))
-            small.append(keep.tile([P, 2, VH], F32, name=f"mn{u}_1", tag=f"shared{u}", align_bytes=64))
+            mn.append(keep.tile([P, 2, VH], F32, name=f"mn{u}_1", tag=f"shared{u}", align_bytes=64))
             if u == 0:
-                gate(2, 4, 0, VH)
+                pool_pairs(2, PACK, 0, VH)
                 quant_z(0, VH)
-                product2(0, 0, VH, "bank0_0", ends_early[:])
+                second_product(0, 0, VH, "bank0_0", ends_early[:])
             else:
-                gate(2, 3, 0, VH)
-                gate(3, 4, 0, VH // 2)
+                pool_pairs(2, PACK - 1, 0, VH)
+                pool_pairs(PACK - 1, PACK, 0, VH // 2)
                 quant_z(0, VH // 2)
-                gate(3, 4, VH // 2, VH)
+                pool_pairs(PACK - 1, PACK, VH // 2, VH)
                 w_late = round_w(1, nc.scalar.copy, "shared1")
                 quant_z(VH // 2, VH)
 
         out_rows = out.rearrange("(p t) v -> p t v", t=PACK)
         ends = keep.tile([P, PACK, 2], F32, name="ends")
         shifts = keep.tile([P, PACK, 2], F32, name="shifts")
-        product2(0, VH, V, f"bank0_{HALF}", ends[:, 0])
+        second_product(0, VH, V, f"bank0_{SH}", ends[:, 0])
         for e, op in enumerate([ALU.max, ALU.min]):
             nc.vector.scalar_tensor_tensor(
-                shifts[:, 0, e : e + 1], ends[:, 0, e : e + 1], ends_early[:, e : e + 1], minus_rates[:, 0, e : e + 1], op, ALU.mult
+                shifts[:, 0, e : e + 1],
+                ends[:, 0, e : e + 1],
+                ends_early[:, e : e + 1],
+                minus_rates[:, 0, e : e + 1],
+                op,
+                ALU.mult,
             )
         for t in range(1, PACK):
-            if t == 2:
+            if t == PACK // 2:
                 quant_w(1, w_late)
-            product2(t, 0, V, f"bank{t}_0", ends[:, t])
+            second_product(t, 0, V, f"bank{t}_0", ends[:, t])
             nc.vector.tensor_tensor(shifts[:, t], ends[:, t], minus_rates[:, t], ALU.mult)
+
         for t in range(PACK):
             ea = keep.tile([P, V], F32, name=f"ea{t}")
-            eb = keep.tile([P, V], F32, name=f"eb{t}")
+            ea2 = keep.tile([P, V], F32, name=f"ea2_{t}")
             both = keep.tile([P, V], F32, name=f"both{t}")
             res = keep.tile([P, V], F32, name=f"res{t}")
-            parts = 2 if t == PACK - 1 else 1
-            width = V // parts
-            for s in range(parts):
-                cols = slice(s * width, (s + 1) * width)
-                lcols = slice(s * width // LIST_COL, (s + 1) * width // LIST_COL)
+            width = VH if t == PACK - 1 else V
+            for lo in range(0, V, width):
+                cols = slice(lo, lo + width)
+                entries = slice(lo // LIST_COL, (lo + width) // LIST_COL)
                 nc.scalar.activation(
-                    ea[:, cols], h2_win[t][:].indirect(n2_t[:, lcols]), ACT.Exp,
-                    bias=shifts[:, t, 0:1], scale=rates[:, t, 0:1],
+                    ea[:, cols],
+                    h2_win[t][:].indirect(n2_t[:, entries]),
+                    ACT.Exp,
+                    bias=shifts[:, t, 0:1],
+                    scale=rates[:, t, 0:1],
                 )
                 nc.scalar.activation(
-                    eb[:, cols], h2_win[t][:].indirect(n3_t[:, lcols]), ACT.Exp,
-                    bias=shifts[:, t, 1:2], scale=rates[:, t, 1:2],
+                    ea2[:, cols],
+                    h2_win[t][:].indirect(n3_t[:, entries]),
+                    ACT.Exp,
+                    bias=shifts[:, t, 1:2],
+                    scale=rates[:, t, 1:2],
                 )
-                nc.vector.tensor_tensor(both[:, cols], ea[:, cols], eb[:, cols], ALU.add)
-                nc.vector.scalar_tensor_tensor(res[:, cols], both[:, cols], 1.5, h2_win[t][:, cols], ALU.mult, ALU.mult)
+                nc.vector.tensor_tensor(both[:, cols], ea[:, cols], ea2[:, cols], ALU.add)
+                nc.vector.scalar_tensor_tensor(
+                    res[:, cols], both[:, cols], 1.5, h2_win[t][:, cols], ALU.mult, ALU.mult
+                )
                 nc.sync.dma_start(out_rows[:, t, cols], res[:, cols])

from contextlib import ExitStack

import concourse.mybir as mybir

K, T, S, V, N, G, H = 512, 2048, 512, 256, 512, 2048, 512
FLOPS = 2 * K * H * S + 2 * H * N * V

F32 = mybir.dt.float32
BF16 = mybir.dt.bfloat16
I32 = mybir.dt.int32
U32 = mybir.dt.uint32
U16 = mybir.dt.uint16
U8 = mybir.dt.uint8
FP8X4 = mybir.dt.float8_e4m3fn_x4
ALU = mybir.AluOpType
ACT = mybir.ActivationFunctionType
AX = mybir.AxisListType

P = 128
PACK = 4
LIST_COL = 16
BLOCK_PARTS = 8
QUAD = 32
LINE = 4
SH = S // 2
VH = V // 2


def tile_picked_hpqhpgateedf_none_p_kernel(
    tc, x_words, x_scales, d_words, d_scales, gn, w1, tau, tau2, offs, k1, n1, n2, n3, out
):
    nc = tc.nc
    with ExitStack() as ctx:
        lists = ctx.enter_context(tc.tile_pool(name="lists", bufs=1))
        keep = ctx.enter_context(tc.tile_pool(name="keep", bufs=1))
        psum = ctx.enter_context(tc.psum_pool(name="psum", bufs=1))

        k1_t = lists.tile([P, H // LIST_COL], U16, name="k1_t")
        offs_t = lists.tile([P, S // LIST_COL], U16, name="offs_t")
        n1_t = lists.tile([P, S // LIST_COL], U16, name="n1_t")
        n2_t = lists.tile([P, V // LIST_COL], U16, name="n2_t")
        n3_t = lists.tile([P, V // LIST_COL], U16, name="n3_t")

        d_sc_tab = keep.tile([P, G], U8, name="d_sc_tab", align_bytes=64)
        x_sc_tab = keep.tile([P, T], U8, name="x_sc_tab", align_bytes=64)
        d_tab = keep.tile([P, G], U32, name="d_tab", align_bytes=64)
        x_tab = keep.tile([P, T], U32, name="x_tab", align_bytes=64)
        planes = keep.tile([P, H + S], U8, name="planes", align_bytes=64)
        gn_t = keep.tile([P, PACK], F32, name="gn_t")
        tau_t = keep.tile([P, PACK], F32, name="tau_t")
        tau2_t = keep.tile([P, PACK], F32, name="tau2_t")

        nc.vector.memset(x_sc_tab[:].bitcast(I32), 0)
        nc.vector.memset(d_sc_tab[:].bitcast(I32), 0)
        nc.sync.dma_start(offs_t[:], offs)
        nc.sync.dma_start(x_sc_tab[:].bitcast(I32)[0:P:BLOCK_PARTS, :], x_scales[0].bitcast(I32))
        nc.sync.dma_start(k1_t[:], k1)
        nc.sync.dma_start(d_sc_tab[:].bitcast(I32)[0:P:BLOCK_PARTS, :], d_scales[0].bitcast(I32))
        nc.sync.dma_start(n1_t[:], n1)
        nc.sync.dma_start(n2_t[:], n2)
        nc.sync.dma_start(d_tab[:].bitcast(I32), d_words[0].rearrange("p n t -> p (n t)").bitcast(I32))
        nc.sync.dma_start(x_tab[:].bitcast(I32), x_words[0].rearrange("p n t -> p (n t)").bitcast(I32))
        nc.sync.dma_start(n3_t[:], n3)
        nc.gpsimd.dma_start(gn_t[:], gn.rearrange("(p t) o -> p (t o)", t=PACK))
        nc.gpsimd.dma_start(tau_t[:], tau.rearrange("(p t) o -> p (t o)", t=PACK))
        nc.gpsimd.dma_start(tau2_t[:], tau2.rearrange("(p t) o -> p (t o)", t=PACK))
        nc.vector.memset(planes[:].bitcast(I32), 0)

        h2_win = [keep.tile([P, 2 * V], F32, name=f"h2_win{t}", align_bytes=64) for t in range(PACK)]
        for t in range(PACK):
            nc.vector.memset(h2_win[t][:, V:], 0.0)

        half_gn = keep.tile([P, PACK], F32, name="half_gn")
        rates = keep.tile([P, PACK, 2], F32, name="rates")
        nc.gpsimd.tensor_scalar(half_gn[:], gn_t[:], 0.5, 0.0, ALU.mult, ALU.add)
        nc.gpsimd.tensor_copy(rates[:, :, 0], tau_t[:])
        nc.gpsimd.tensor_scalar(rates[:, :, 1], tau2_t[:], -1.0, 0.0, ALU.mult, ALU.add)
        minus_rates = keep.tile([P, PACK, 2], F32, name="minus_rates")
        nc.gpsimd.tensor_scalar(minus_rates[:], rates[:], -1.0, 0.0, ALU.mult, ALU.add)

        d_sc = keep.tile([P, H], U8, name="d_sc", tag="d_sc", align_bytes=64)
        x_sc = keep.tile([P, S], U8, name="x_sc", tag="x_sc", align_bytes=64)
        staged = keep.tile([P, H + S], U8, name="staged", align_bytes=64)
        nc.vector.tensor_copy(x_sc[:], x_sc_tab[:].indirect(offs_t[:]))
        nc.vector.tensor_copy(d_sc[:], d_sc_tab[:].indirect(k1_t[:]))
        nc.vector.tensor_copy(staged[:, H:].bitcast(I32), x_sc[:].bitcast(I32))
        nc.vector.tensor_copy(
            staged[:, :H].rearrange("p (t m) -> p t m", t=PACK), d_sc[:].rearrange("p (m t) -> p t m", t=PACK)
        )
        for q0 in range(0, P, QUAD):
            nc.sync.dma_start(
                planes[:].bitcast(I32)[q0 : q0 + QUAD // BLOCK_PARTS, :],
                staged[:].bitcast(I32)[q0 : q0 + QUAD : BLOCK_PARTS, :],
            )

        d_pick = keep.tile([P, H], U32, name="d_pick", tag="x_sc", align_bytes=64)
        d_dealt = keep.tile([P, H], U32, name="d_dealt", align_bytes=64)
        x_pick = keep.tile([P, S], U32, name="x_pick", align_bytes=64)
        nc.vector.tensor_copy(d_pick[:], d_tab[:].indirect(k1_t[:]))
        nc.vector.tensor_copy(
            d_dealt[:].bitcast(I32).rearrange("p (t c i) -> p c t i", t=PACK, i=LINE),
            d_pick[:].bitcast(I32).rearrange("p (c i t) -> p c t i", t=PACK, i=LINE),
        )
        w_raw = keep.tile([P, PACK, N], F32, name="w_raw", tag="d_sc", align_bytes=64)
        nc.sync.dma_start(w_raw[:], w1.rearrange("(p j) n -> p j n", j=PACK))
        h_win = [keep.tile([P, S], F32, name=f"h_win{t}", align_bytes=64) for t in range(PACK)]
        for lo in range(0, S, SH):
            nc.vector.tensor_copy(
                x_pick[:, lo : lo + SH], x_tab[:].indirect(offs_t[:, lo // LIST_COL : (lo + SH) // LIST_COL])
            )

        first_halves = [(t, 0, SH) for t in range(2)]
        second_halves = [(t, SH, S) for t in range(2)]
        whole_rows = [(t, 0, S) for t in range(2, PACK)]
        for t, lo, hi in first_halves + second_halves + whole_rows:
            acc = psum.tile([P, hi - lo], F32, name=f"acc{t}_{lo}", tag=f"bank{t}_{lo}")
            nc.tensor.matmul_mx(
                out=acc[:],
                lhsT=d_dealt[:, t * P : (t + 1) * P].bitcast(FP8X4),
                lhsT_scale=planes[:, t * P : (t + 1) * P],
                rhs=x_pick[:, lo:hi].bitcast(FP8X4),
                rhs_scale=planes[:, H + lo : H + hi],
                start=True,
                stop=True,
            )
            if hi == SH:
                nc.scalar.activation(h_win[t][:, lo:hi], acc[:], ACT.Copy, scale=0.0625)
            else:
                nc.vector.tensor_scalar(h_win[t][:, lo:hi], acc[:], 0.0625, None, ALU.mult)

        w_q = keep.tile([P, N], U32, name="w_q", align_bytes=64)
        w_sc = keep.tile([P, N], U8, name="w_sc", align_bytes=64)

        def round_w(a, copy, tag):
            w_bf = keep.tile([P, 2, P, PACK], BF16, name=f"w_bf{a}", tag=tag, align_bytes=64)
            src = w_raw[:].rearrange("p j (c t) -> p c j t", t=PACK)[:, :, :, 2 * a : 2 * a + 2]
            copy(w_bf[:].rearrange("p t c j -> p c j t"), src)
            return w_bf

        def quant_w(a, w_bf):
            nc.vector.quantize_mx(
                out=w_q[:, 2 * a * P : (2 * a + 2) * P].bitcast(FP8X4),
                scales=w_sc[:, 2 * a * P : (2 * a + 2) * P],
                in_=w_bf[:].rearrange("p t c j -> p (t c j)"),
            )

        z_q = keep.tile([P, V], U32, name="z_q", align_bytes=64)
        z_sc = keep.tile([P, V], U8, name="z_sc", align_bytes=64)

        def second_product(t, lo, hi, bank, top_low):
            acc2 = psum.tile([P, hi - lo], F32, name=f"acc2_{t}_{lo}", tag=bank)
            nc.tensor.matmul_mx(
                out=acc2[:],
                lhsT=w_q[:, t * P : (t + 1) * P].bitcast(FP8X4),
                lhsT_scale=w_sc[:, t * P : (t + 1) * P],
                rhs=z_q[:, lo:hi].bitcast(FP8X4),
                rhs_scale=z_sc[:, lo:hi],
                start=True,
                stop=True,
            )
            nc.vector.tensor_scalar(
                h2_win[t][:, lo:hi], acc2[:], 1.0, None, ALU.mult, ALU.max, accum_out=top_low[:, 0:1]
            )
            nc.vector.tensor_reduce(top_low[:, 1:2], acc2[:], AX.X, ALU.min)

        ends_early = keep.tile([P, 2], F32, name="ends_early")
        for u in range(2):
            ln = [
                keep.tile([P, 2, VH, 2], F32, name=f"ln{u}_{two}", tag=f"ln{two}", align_bytes=64) for two in range(2)
            ]
            mx = keep.tile([P, PACK, VH], F32, name=f"mx{u}", align_bytes=64)
            th = keep.tile([P, PACK, VH], F32, name=f"th{u}", align_bytes=64)
            gate = keep.tile([P, PACK, VH], F32, name=f"gate{u}", align_bytes=64)
            z_bf = keep.tile([P, VH, PACK], BF16, name=f"z_bf{u}", align_bytes=64)

            def pool_pairs(a, b, lo, hi):
                first = 2 * (u * VH + lo) // LIST_COL
                n1_cols = n1_t[:, first : first + 2 * (hi - lo) // LIST_COL]
                for t in range(a, b):
                    nc.scalar.activation(
                        ln[t // 2][:, t % 2, lo:hi].rearrange("p v e -> p (v e)"),
                        h_win[t][:].indirect(n1_cols),
                        ACT.Copy,
                    )
                pairs = ln[a // 2][:, a % 2 : a % 2 + b - a, lo:hi]
                smaller = mn[a // 2][:, a % 2 : a % 2 + b - a, lo:hi]
                nc.vector.tensor_tensor(smaller, pairs[:, :, :, 0], pairs[:, :, :, 1], ALU.min)
                nc.vector.tensor_tensor(mx[:, a:b, lo:hi], pairs[:, :, :, 0], pairs[:, :, :, 1], ALU.max)
                nc.scalar.activation(th[:, a:b, lo:hi], smaller, ACT.Tanh, scale=0.5)
                for t in range(a, b):
                    g = half_gn[:, t : t + 1]
                    nc.vector.tensor_scalar(gate[:, t, lo:hi], th[:, t, lo:hi], g, g, ALU.mult, ALU.add)

            def quant_z(lo, hi):
                nc.vector.tensor_tensor(
                    z_bf[:, lo:hi].rearrange("p (c i) t -> p c t i", i=LINE),
                    gate[:, :, lo:hi].rearrange("p t (c i) -> p c t i", i=LINE),
                    mx[:, :, lo:hi].rearrange("p t (c i) -> p c t i", i=LINE),
                    ALU.mult,
                )
                nc.vector.quantize_mx(
                    out=z_q[:, u * VH + lo : u * VH + hi].bitcast(FP8X4),
                    scales=z_sc[:, u * VH + lo : u * VH + hi],
                    in_=z_bf[:, lo:hi].rearrange("p v t -> p (v t)"),
                )

            mn = [keep.tile([P, 2, VH], F32, name=f"mn{u}_0", align_bytes=64)]
            pool_pairs(0, 2, 0, VH)
            if u == 0:
                quant_w(0, round_w(0, nc.vector.tensor_copy, "shared0"))
            mn.append(keep.tile([P, 2, VH], F32, name=f"mn{u}_1", tag=f"shared{u}", align_bytes=64))
            if u == 0:
                pool_pairs(2, PACK, 0, VH)
                quant_z(0, VH)
                second_product(0, 0, VH, "bank0_0", ends_early[:])
            else:
                pool_pairs(2, PACK - 1, 0, VH)
                pool_pairs(PACK - 1, PACK, 0, VH // 2)
                quant_z(0, VH // 2)
                pool_pairs(PACK - 1, PACK, VH // 2, VH)
                w_late = round_w(1, nc.scalar.copy, "shared1")
                quant_z(VH // 2, VH)

        out_rows = out.rearrange("(p t) v -> p t v", t=PACK)
        ends = keep.tile([P, PACK, 2], F32, name="ends")
        shifts = keep.tile([P, PACK, 2], F32, name="shifts")
        second_product(0, VH, V, f"bank0_{SH}", ends[:, 0])
        for e, op in enumerate([ALU.max, ALU.min]):
            nc.vector.scalar_tensor_tensor(
                shifts[:, 0, e : e + 1],
                ends[:, 0, e : e + 1],
                ends_early[:, e : e + 1],
                minus_rates[:, 0, e : e + 1],
                op,
                ALU.mult,
            )
        for t in range(1, PACK):
            if t == PACK // 2:
                quant_w(1, w_late)
            second_product(t, 0, V, f"bank{t}_0", ends[:, t])
            nc.vector.tensor_tensor(shifts[:, t], ends[:, t], minus_rates[:, t], ALU.mult)

        for t in range(PACK):
            ea = keep.tile([P, V], F32, name=f"ea{t}")
            ea2 = keep.tile([P, V], F32, name=f"ea2_{t}")
            both = keep.tile([P, V], F32, name=f"both{t}")
            res = keep.tile([P, V], F32, name=f"res{t}")
            width = VH if t == PACK - 1 else V
            for lo in range(0, V, width):
                cols = slice(lo, lo + width)
                entries = slice(lo // LIST_COL, (lo + width) // LIST_COL)
                nc.scalar.activation(
                    ea[:, cols],
                    h2_win[t][:].indirect(n2_t[:, entries]),
                    ACT.Exp,
                    bias=shifts[:, t, 0:1],
                    scale=rates[:, t, 0:1],
                )
                nc.scalar.activation(
                    ea2[:, cols],
                    h2_win[t][:].indirect(n3_t[:, entries]),
                    ACT.Exp,
                    bias=shifts[:, t, 1:2],
                    scale=rates[:, t, 1:2],
                )
                nc.vector.tensor_tensor(both[:, cols], ea[:, cols], ea2[:, cols], ALU.add)
                nc.vector.scalar_tensor_tensor(
                    res[:, cols], both[:, cols], 1.5, h2_win[t][:, cols], ALU.mult, ALU.mult
                )
                nc.sync.dma_start(out_rows[:, t, cols], res[:, cols])
